import numpy as np
import ml_dtypes


def mxq(x, axis, fmt="e4m3"):
    dtype, down = {"e4m3": (ml_dtypes.float8_e4m3fn, 7), "e5m2": (ml_dtypes.float8_e5m2, 14)}[fmt]
    v = np.moveaxis(np.asarray(x, np.float32).astype(ml_dtypes.bfloat16).astype(np.float64), axis, -1)
    blocks = v.reshape(v.shape[:-1] + (-1, 32))
    amax = np.abs(blocks).max(-1, keepdims=True)
    byte = np.maximum(np.where(amax > 0, np.frexp(amax)[1] - 1 + 127, 0) - down, 1)
    scale = np.exp2(byte - 127.0)
    codes = (blocks / scale).astype(np.float32).astype(dtype).astype(np.float64)
    return np.moveaxis((codes * scale).reshape(v.shape), -1, axis)


WIDE = False


def mx_kscale(k):
    if not WIDE:
        return np.ones(k)
    levels = np.array([10, -10, 5, -5, 0])
    if k % 512:
        return np.exp2(np.random.permutation(np.resize(levels, k // 32))).repeat(32)
    a = np.empty((k // 512, 16))
    for p in range(k // 512):
        a[p, :8] = np.random.permutation(np.resize(levels, 8))
        for g in range(8):
            far = levels[np.abs(levels - a[p, g]) >= 10]
            a[p, g + 8] = far[np.random.randint(len(far))]
    return np.exp2(a.ravel()).repeat(32)


BF16 = ml_dtypes.bfloat16


def bf(x):
    return np.asarray(x, np.float32).astype(BF16)


def f64(x):
    return np.asarray(x).astype(np.float64)


E2M1 = np.array([0.0, 0.5, 1.0, 1.5, 2.0, 3.0, 4.0, 6.0, -0.0, -0.5, -1.0, -1.5, -2.0, -3.0, -4.0, -6.0])


def pack_weight(w, fmt):
    k, n = w.shape
    w = f64(bf(w)).reshape(k // 32, 32, n)
    amax = np.abs(w).max(1)
    if fmt == "e4m3":
        byte = np.frexp(amax)[1] - 1 + 127 - 7
    else:
        mant, ex = np.frexp(amax / 6.0)
        byte = np.where(mant > 0.5, ex, ex - 1) + 127
    byte = np.clip(np.where(amax > 0, byte, 1), 1, 254)
    scaled = (w * np.exp2(127.0 - byte)[:, None, :]).reshape(k, n).astype(np.float32)
    by_word = np.ascontiguousarray(scaled.reshape(k // 512, 128, 4, n).transpose(0, 1, 3, 2))
    if fmt == "e4m3":
        words = by_word.astype(ml_dtypes.float8_e4m3fn).view(np.uint8)
    else:
        c = by_word.astype(ml_dtypes.float4_e2m1fn).view(np.uint8) & 0xF
        words = c[..., 0::2] | (c[..., 1::2] << 4)
    return np.ascontiguousarray(words), np.ascontiguousarray(byte.astype(np.uint8).reshape(k // 512, 16, n))


def unpack_weight(words, scales, fmt):
    g, p, n, _ = words.shape
    if fmt == "e4m3":
        vals = np.ascontiguousarray(words).view(ml_dtypes.float8_e4m3fn).astype(np.float64)
    else:
        nib = np.empty((g, p, n, 4), np.uint8)
        nib[..., 0::2] = words & 0xF
        nib[..., 1::2] = words >> 4
        vals = E2M1[nib]
    vals = vals * np.repeat(np.exp2(scales.astype(np.float64) - 127.0), 8, axis=1)[..., None]
    return vals.transpose(0, 1, 3, 2).reshape(g * 512, n)
def pack4(w):
    words, scales = pack_weight(w, "e2m1")
    return words.reshape(words.shape[0], 128, -1), scales


def unpack4(words, scales):
    return unpack_weight(words.reshape(words.shape[0], 128, -1, 2), scales, "e2m1")


M, K, F, N, R = 1024, 1024, 2048, 1024, 128


def draw0():
    s, t, u = mx_kscale(K), mx_kscale(F), mx_kscale(M)
    x = np.random.standard_normal((M, K)) * s * u[:, None]
    w_up = np.random.standard_normal((K, F)) / np.sqrt(K) / s[:, None] * t
    gate = 1.4 * np.random.standard_normal((M, F))
    w_down = np.random.standard_normal((F, N)) / np.sqrt(F) / t[:, None]
    lora_a = np.random.standard_normal((F, R)) / np.sqrt(F) / t[:, None]
    dz = np.random.standard_normal((M, R)) / np.sqrt(M) / u[:, None]
    down_words, down_scales = pack4(w_down)
    return {"x": bf(x), "w_up": bf(w_up), "gate": bf(gate),
            "down_words": down_words, "down_scales": down_scales,
            "lora_a": bf(lora_a), "dz": bf(dz)}


def core(x, w_up, gate, down_words, down_scales, lora_a, dz):
    up = mxq(f64(x), 1, "e4m3") @ mxq(f64(w_up), 0, "e4m3")
    h = np.maximum(f64(gate), 0.0) * up
    h_f = mxq(h, 1, "e4m3")
    h_m = mxq(h, 0, "e4m3")
    y = h_f @ unpack4(down_words, down_scales)
    z = h_f @ mxq(f64(lora_a), 0, "e4m3")
    da = h_m.T @ mxq(f64(dz), 0, "e4m3")
    return y, z, da


def e4m3fn_bytes(y):
    return np.clip(np.asarray(y, np.float64), -448.0, 448.0).astype(np.float32).astype(ml_dtypes.float8_e4m3fn).view(np.uint8)


def e4m3fn_values(b):
    return np.asarray(b, np.uint8).view(ml_dtypes.float8_e4m3fn).astype(np.float64)


def setup_inputs():
    d = draw0()
    x0 = np.asarray(d['lora_a']).astype(np.float64)
    s = (np.max(np.abs(x0), axis=(1,), keepdims=True) / 448.0).astype(np.float32)
    out = {}
    for k, v in d.items():
        if k == 'lora_a':
            out['lora_a_bytes'] = e4m3fn_bytes(x0 / s.astype(np.float64))
            out['lora_a_scale'] = s
        else:
            out[k] = v
    return out


def reference(x, w_up, gate, down_words, down_scales, lora_a_bytes, lora_a_scale, dz):
    return core(x, w_up, gate, down_words, down_scales, e4m3fn_values(lora_a_bytes) * lora_a_scale.astype(np.float64), dz)

@@ -1,0 +1,449 @@
+from contextlib import ExitStack
+
+import concourse.mybir as mybir
+from concourse.masks import make_identity
+
+M, K, F, N, R = 1024, 1024, 2048, 1024, 128
+FLOPS = 2 * M * K * F + 2 * M * F * N + 4 * M * F * R
+
+F32 = mybir.dt.float32
+BF16 = mybir.dt.bfloat16
+I32 = mybir.dt.int32
+U32 = mybir.dt.uint32
+U8 = mybir.dt.uint8
+FP8 = mybir.dt.float8_e4m3fn
+FP8X4 = mybir.dt.float8_e4m3fn_x4
+FP4X4 = mybir.dt.float4_e2m1fn_x4
+ALU = mybir.AluOpType
+COPY = mybir.ActivationFunctionType.Copy
+
+P = 128
+GM = 512
+GF = 512
+BLOCKS = [(0, 0), (0, 1), (1, 0), (1, 1), (2, 0), (3, 0), (2, 1), (3, 1)]
+
+
+def tile_qlora_down_projection_s8_kernel(
+    tc, x, w_up, gate, down_words, down_scales, lora_a_bytes, lora_a_scale, dz, y, z, da
+):
+    nc = tc.nc
+    with ExitStack() as ctx:
+        keep = ctx.enter_context(tc.tile_pool(name="keep", bufs=1))
+        work = ctx.enter_context(tc.tile_pool(name="work", bufs=2))
+        psum = ctx.enter_context(tc.psum_pool(name="psum", bufs=2))
+
+        def kept(name, shape, dtype):
+            return keep.tile(shape, dtype, name=name, align_bytes=64)
+
+        ident = kept("ident", [P, P], F32)
+        make_identity(nc, ident[:])
+        dsc = kept("dsc", [P, 4, N], U8)
+        nc.gpsimd.memset(dsc[:].rearrange("p g n -> p (g n)").bitcast(I32), 0)
+
+        x_raw = [kept("x_raw%d" % g, [P, 4, K], BF16) for g in range(2)]
+        w_raw = {(G, c): kept("w_raw%d%d" % (G, c), [P, 4, GF], BF16) for G in range(4) for c in range(2)}
+        gate_sb = {b: kept("gate%d%d" % b, [P, 4, GF], BF16) for b in BLOCKS}
+        words = kept("words", [P, 4, 2 * N], U8)
+        lbytes = kept("lbytes", [P, 4, 4 * R], U8)
+        lscale = kept("lscale", [P, 16], F32)
+        dz_raw = kept("dz_raw", [P, 2, 4 * R], BF16)
+
+        xv = x.rearrange("(g p s) k -> g p s k", p=P, s=4)
+        wv = w_up.rearrange("(c p j) f -> c p j f", p=P, j=4)
+        gv = gate.rearrange("(g p s) f -> g p s f", p=P, s=4)
+
+        def load_x(g, s):
+            nc.sync.dma_start(out=x_raw[g][:, s, :], in_=xv[g, :, s, :])
+
+        def load_w(G, c, f0, f1):
+            nc.sync.dma_start(out=w_raw[G, c][:, :, f0:f1], in_=wv[c, :, :, G * GF + f0 : G * GF + f1])
+
+        def load_gate(G, g):
+            nc.sync.dma_start(out=gate_sb[G, g][:], in_=gv[g, :, :, G * GF : (G + 1) * GF])
+
+        load_w(0, 0, 0, 512)
+        load_x(0, 0)
+        load_w(0, 1, 0, 512)
+        load_x(0, 1)
+        load_x(0, 2)
+        load_x(0, 3)
+        load_gate(0, 0)
+        for s in range(4):
+            load_x(1, s)
+        load_gate(0, 1)
+        load_w(1, 0, 0, 512)
+        load_w(1, 1, 0, 512)
+        load_gate(1, 0)
+        load_gate(1, 1)
+        load_w(2, 0, 0, 512)
+        load_w(2, 1, 0, 512)
+        load_gate(2, 0)
+        load_w(3, 0, 0, 512)
+        load_w(3, 1, 0, 512)
+        load_gate(3, 0)
+        nc.sync.dma_start(out=dz_raw[:], in_=dz.rearrange("(g p t) r -> p g (t r)", p=P, t=4))
+        for Q in range(4):
+            nc.sync.dma_start(
+                out=dsc[32 * Q : 32 * Q + 4, :, :].bitcast(I32),
+                in_=down_scales[:, 4 * Q : 4 * Q + 4, :].bitcast(I32).rearrange("g q w -> q g w"),
+            )
+        nc.sync.dma_start(out=words[:], in_=down_words.rearrange("g p w -> p g w"))
+        load_gate(2, 1)
+        nc.sync.dma_start(out=lbytes[:], in_=lora_a_bytes.rearrange("(g p t) r -> p g (t r)", p=P, t=4))
+        nc.sync.dma_start(
+            out=lscale[:].rearrange("p (g t) -> p g t", t=4),
+            in_=lora_a_scale.rearrange("(g p t) o -> p g (t o)", p=P, t=4),
+        )
+        load_gate(3, 1)
+
+        x_codes = {(g, s): kept("xc%d%d" % (g, s), [P, 2 * P], U32) for g in range(2) for s in range(4)}
+        x_scales = {(g, s): kept("xs%d%d" % (g, s), [P, 2 * P], U8) for g in range(2) for s in range(4)}
+        w_codes = {(G, c): kept("wc%d%d" % (G, c), [P, GF], U32) for G in range(4) for c in range(2)}
+        w_scales = {(G, c): kept("ws%d%d" % (G, c), [P, GF], U8) for G in range(4) for c in range(2)}
+        hm_codes = {b: kept("hmc%d%d" % b, [P, GF], U32) for b in BLOCKS}
+        hm_scales = {b: kept("hms%d%d" % b, [P, GF], U8) for b in BLOCKS}
+        hf_codes = {b: kept("hfc%d%d" % b, [P, GM], U32) for b in BLOCKS}
+        hf_scales = {b: kept("hfs%d%d" % b, [P, GM], U8) for b in BLOCKS}
+        dz_codes = kept("dzc", [P, 2 * R], U32)
+        dz_scales = kept("dzs", [P, 2 * R], U8)
+        la_codes = kept("lac", [P, 4 * R], U32)
+        la_scales = kept("las", [P, 4 * R], U8)
+
+        def copy_on(engine, out, in_):
+            if engine == "V":
+                nc.vector.tensor_copy(out=out, in_=in_)
+            else:
+                nc.scalar.copy(out=out, in_=in_)
+
+        xg = {}
+
+        def x_turn(g, s, engine):
+            bank = psum.tile([P, 4, P], F32, name="tr", bufs=2)
+            xw = x_raw[g][:, s, :].bitcast(F32)
+            for c in range(2):
+                for u in range(2):
+                    nc.tensor.transpose(bank[:, 2 * c + u, :], xw[:, 256 * c + u : 256 * (c + 1) : 2], ident[:])
+            t = work.tile([P, 2 * P * 4], BF16, name="xg", bufs=2, align_bytes=64)
+            copy_on(
+                engine,
+                t[:].bitcast(F32).rearrange("p (c q u) -> p c q u", c=2, u=2),
+                bank[:].rearrange("p (c u) q -> p c q u", c=2),
+            )
+            xg[g, s] = t
+
+        def x_quant(g, s):
+            nc.vector.quantize_mx(out=x_codes[g, s][:].bitcast(FP8X4), scales=x_scales[g, s][:], in_=xg[g, s][:])
+
+        wg = {}
+
+        def w_mix(G, c, half, engine):
+            if half == 0:
+                wt = work.tile([P, GF * 4], BF16, name="wg", bufs=4, align_bytes=64)
+                wg[G, c] = wt
+            t = wg[G, c][:, 1024 * half : 1024 * (half + 1)]
+            src = w_raw[G, c][:]
+            copy_on(
+                engine,
+                t.rearrange("p (t q j) -> p t q j", t=2, j=4),
+                src.rearrange("p j (q t) -> p t q j", t=4)[:, 2 * half : 2 * half + 2],
+            )
+
+        def w_quant(G, c, f0, f1):
+            nc.vector.quantize_mx(
+                out=w_codes[G, c][:, f0:f1].bitcast(FP8X4),
+                scales=w_scales[G, c][:, f0:f1],
+                in_=wg[G, c][:, 4 * f0 : 4 * f1],
+            )
+
+        up_bank = {}
+        h_tile = {}
+
+        def up(b, i):
+            G, g = b
+            bank = psum.tile([P, 4, P], F32, name="up", bufs=3)
+            fs = slice(128 * i, 128 * (i + 1))
+            for s in range(4):
+                for c in range(2):
+                    ks = slice(P * c, P * (c + 1))
+                    nc.tensor.matmul_mx(
+                        out=bank[:, s, :],
+                        lhsT=x_codes[g, s][:, ks].bitcast(FP8X4),
+                        lhsT_scale=x_scales[g, s][:, ks],
+                        rhs=w_codes[G, c][:, fs].bitcast(FP8X4),
+                        rhs_scale=w_scales[G, c][:, fs],
+                        start=(c == 0),
+                        stop=(c == 1),
+                    )
+            up_bank[b, i] = bank
+
+        def h_mul(b, i):
+            if i == 0:
+                ht = work.tile([P, GF * 4], BF16, name="h", bufs=5, align_bytes=64)
+                h_tile[b] = ht
+            nc.vector.scalar_tensor_tensor(
+                out=h_tile[b][:].rearrange("p (t q s) -> p t q s", t=4, s=4)[:, i],
+                in0=gate_sb[b][:].rearrange("p s (q t) -> p t q s", t=4)[:, i],
+                scalar=0.0,
+                in1=up_bank[b, i][:].rearrange("p s q -> p q s"),
+                op0=ALU.max,
+                op1=ALU.mult,
+            )
+
+        def hm_quant(b):
+            nc.vector.quantize_mx(out=hm_codes[b][:].bitcast(FP8X4), scales=hm_scales[b][:], in_=h_tile[b][:])
+
+        hf_tile = {}
+
+        def h_turn(b, engines):
+            hw = h_tile[b][:].bitcast(F32)
+            hft = work.tile([P, GM * 4], BF16, name="hf", bufs=2, align_bytes=64)
+            hf_tile[b] = hft
+            for u in range(2):
+                bank = psum.tile([P, 4, P], F32, name="tr", bufs=2)
+                for t in range(4):
+                    nc.tensor.transpose(bank[:, t, :], hw[:, 256 * t + u : 256 * (t + 1) : 2], ident[:])
+                copy_on(
+                    engines[u],
+                    hft[:].rearrange("p (u e q t) -> p u e q t", u=2, e=2, t=4)[:, u],
+                    bank[:].bitcast(BF16).rearrange("p t (q e) -> p e q t", e=2),
+                )
+
+        def hf_quant(b):
+            nc.vector.quantize_mx(out=hf_codes[b][:].bitcast(FP8X4), scales=hf_scales[b][:], in_=hf_tile[b][:])
+
+        def dz_prep():
+            t = work.tile([P, 2 * R * 4], BF16, name="xg", bufs=2, align_bytes=64)
+            for g in range(2):
+                nc.scalar.copy(
+                    out=t[:, 512 * g : 512 * (g + 1)].rearrange("p (r t) -> p r t", t=4),
+                    in_=dz_raw[:, g, :].rearrange("p (t r) -> p r t", t=4),
+                )
+            nc.vector.quantize_mx(out=dz_codes[:].bitcast(FP8X4), scales=dz_scales[:], in_=t[:])
+
+        lora = {}
+
+        def la_widen():
+            t = work.tile([P, 4, 4, R], BF16, name="wg", bufs=4, align_bytes=64)
+            for G in range(4):
+                for j in range(4):
+                    nc.scalar.activation(
+                        out=t[:, G, j, :],
+                        in_=lbytes[:, G, R * j : R * (j + 1)].bitcast(FP8),
+                        func=COPY,
+                        scale=lscale[:, 4 * G + j : 4 * G + j + 1],
+                    )
+            lora[0] = t
+
+        def la_quant():
+            t = work.tile([P, 4 * R * 4], BF16, name="wg", bufs=4, align_bytes=64)
+            nc.vector.tensor_copy(
+                out=t[:].rearrange("p (g r j) -> p g r j", g=4, j=4), in_=lora[0][:].rearrange("p g j r -> p g r j")
+            )
+            nc.vector.quantize_mx(out=la_codes[:].bitcast(FP8X4), scales=la_scales[:], in_=t[:])
+
+        yv = y.rearrange("(g q s) n -> g s q n", q=P, s=4)
+        zv = z.rearrange("(g q s) r -> g q s r", q=P, s=4)
+        dav = da.rearrange("(g q t) r -> g q t r", q=P, t=4)
+
+        def y_out(g, s, half, engine):
+            bank = psum.tile([P, 512], F32, name="acc", bufs=3)
+            ns = slice(512 * half, 512 * (half + 1))
+            for G in range(4):
+                nc.tensor.matmul_mx(
+                    out=bank[:],
+                    lhsT=hf_codes[G, g][:, P * s : P * (s + 1)].bitcast(FP8X4),
+                    lhsT_scale=hf_scales[G, g][:, P * s : P * (s + 1)],
+                    rhs=words[:, G, 1024 * half : 1024 * (half + 1)].bitcast(FP4X4),
+                    rhs_scale=dsc[:, G, ns],
+                    start=(G == 0),
+                    stop=(G == 3),
+                )
+            t = work.tile([P, 512], F32, name="yo", bufs=5)
+            copy_on(engine, t[:], bank[:])
+            nc.sync.dma_start(out=yv[g, s, :, ns], in_=t[:])
+
+        def z_out(g, engine):
+            bank = psum.tile([P, 4, R], F32, name="acc", bufs=3)
+            for s in range(4):
+                for G in range(4):
+                    nc.tensor.matmul_mx(
+                        out=bank[:, s, :],
+                        lhsT=hf_codes[G, g][:, P * s : P * (s + 1)].bitcast(FP8X4),
+                        lhsT_scale=hf_scales[G, g][:, P * s : P * (s + 1)],
+                        rhs=la_codes[:, R * G : R * (G + 1)].bitcast(FP8X4),
+                        rhs_scale=la_scales[:, R * G : R * (G + 1)],
+                        start=(G == 0),
+                        stop=(G == 3),
+                    )
+            t = work.tile([P, 4, R], F32, name="yo", bufs=5)
+            copy_on(engine, t[:], bank[:])
+            nc.sync.dma_start(out=zv[g], in_=t[:])
+
+        def da_out(G, engine):
+            bank = psum.tile([P, 4, R], F32, name="acc", bufs=3)
+            for t in range(4):
+                for g in range(2):
+                    nc.tensor.matmul_mx(
+                        out=bank[:, t, :],
+                        lhsT=hm_codes[G, g][:, P * t : P * (t + 1)].bitcast(FP8X4),
+                        lhsT_scale=hm_scales[G, g][:, P * t : P * (t + 1)],
+                        rhs=dz_codes[:, R * g : R * (g + 1)].bitcast(FP8X4),
+                        rhs_scale=dz_scales[:, R * g : R * (g + 1)],
+                        start=(g == 0),
+                        stop=(g == 1),
+                    )
+            t = work.tile([P, 4, R], F32, name="yo", bufs=5)
+            copy_on(engine, t[:], bank[:])
+            nc.sync.dma_start(out=dav[G], in_=t[:])
+
+        def y_next(g, engines):
+            for e in engines:
+                s, half = y_todo[g].pop(0)
+                y_out(g, s, half, e)
+
+        y_todo = {g: [(s, half) for s in range(4) for half in range(2)] for g in range(2)}
+        w_mix(0, 0, 0, "V")
+        w_mix(0, 0, 1, "S")
+        x_turn(0, 0, "S")
+        w_quant(0, 0, 0, 512)
+        w_mix(0, 1, 0, "V")
+        w_mix(0, 1, 1, "S")
+        x_quant(0, 0)
+        x_turn(0, 1, "V")
+        w_quant(0, 1, 0, 512)
+        x_turn(0, 2, "S")
+        x_quant(0, 1)
+        x_turn(0, 3, "S")
+        x_quant(0, 2)
+        x_quant(0, 3)
+        x_turn(1, 0, "S")
+        up(BLOCKS[0], 0)
+        h_mul(BLOCKS[0], 0)
+        x_turn(1,1,"S")
+        x_quant(1,0)
+        up(BLOCKS[0], 1)
+        h_mul(BLOCKS[0], 1)
+        x_turn(1,2,"S")
+        x_quant(1,1)
+        up(BLOCKS[0], 2)
+        h_mul(BLOCKS[0], 2)
+        x_turn(1,3,"S")
+        x_quant(1,2)
+        up(BLOCKS[0], 3)
+        h_mul(BLOCKS[0], 3)
+        x_quant(1,3)
+        w_mix(1,0,0,"S")
+        w_mix(1,0,1,"V")
+        up(BLOCKS[1], 0)
+        h_mul(BLOCKS[1], 0)
+        w_mix(1,1,0,"V")
+        w_quant(1,0,0,512)
+        up(BLOCKS[1], 1)
+        h_mul(BLOCKS[1], 1)
+        h_turn(BLOCKS[0],"SS")
+        w_mix(1,1,1,"S")
+        up(BLOCKS[1], 2)
+        h_mul(BLOCKS[1], 2)
+        w_quant(1,1,0,512)
+        up(BLOCKS[1], 3)
+        h_mul(BLOCKS[1], 3)
+        up(BLOCKS[2], 0)
+        h_mul(BLOCKS[2], 0)
+        hf_quant(BLOCKS[0])
+        w_mix(2,0,0,"S")
+        up(BLOCKS[2], 1)
+        h_mul(BLOCKS[2], 1)
+        h_turn(BLOCKS[1],"SS")
+        w_mix(2,1,0,"V")
+        up(BLOCKS[2], 2)
+        h_mul(BLOCKS[2], 2)
+        w_mix(2,0,1,"S")
+        up(BLOCKS[2], 3)
+        h_mul(BLOCKS[2], 3)
+        w_quant(2,0,0,512)
+        up(BLOCKS[3], 0)
+        h_mul(BLOCKS[3], 0)
+        hf_quant(BLOCKS[1])
+        w_mix(2,1,1,"S")
+        up(BLOCKS[3], 1)
+        h_mul(BLOCKS[3], 1)
+        h_turn(BLOCKS[2],"SS")
+        w_quant(2,1,0,512)
+        up(BLOCKS[3], 2)
+        h_mul(BLOCKS[3], 2)
+        w_mix(3,0,0,"S")
+        w_mix(3,1,0,"V")
+        up(BLOCKS[3], 3)
+        h_mul(BLOCKS[3], 3)
+        w_mix(3,0,1,"S")
+        up(BLOCKS[4], 0)
+        h_mul(BLOCKS[4], 0)
+        hf_quant(BLOCKS[2])
+        w_quant(3,0,0,512)
+        up(BLOCKS[4], 1)
+        h_mul(BLOCKS[4], 1)
+        h_turn(BLOCKS[3],"SS")
+        w_mix(3,1,1,"S")
+        up(BLOCKS[4], 2)
+        h_mul(BLOCKS[4], 2)
+        w_quant(3,1,0,512)
+        up(BLOCKS[4], 3)
+        h_mul(BLOCKS[4], 3)
+        hm_quant(BLOCKS[0])
+        up(BLOCKS[5], 0)
+        h_mul(BLOCKS[5], 0)
+        hf_quant(BLOCKS[3])
+        up(BLOCKS[5], 1)
+        h_mul(BLOCKS[5], 1)
+        h_turn(BLOCKS[4],"SS")
+        up(BLOCKS[5], 2)
+        h_mul(BLOCKS[5], 2)
+        hm_quant(BLOCKS[1])
+        dz_prep()
+        up(BLOCKS[5], 3)
+        h_mul(BLOCKS[5], 3)
+        hm_quant(BLOCKS[2])
+        up(BLOCKS[6], 0)
+        h_mul(BLOCKS[6], 0)
+        hf_quant(BLOCKS[4])
+        up(BLOCKS[6], 1)
+        h_mul(BLOCKS[6], 1)
+        h_turn(BLOCKS[5],"SV")
+        da_out(0,"S")
+        up(BLOCKS[6], 2)
+        h_mul(BLOCKS[6], 2)
+        hm_quant(BLOCKS[3])
+        up(BLOCKS[6], 3)
+        h_mul(BLOCKS[6], 3)
+        hf_quant(BLOCKS[5])
+        da_out(1,"S")
+        y_next(0,"VS")
+        la_widen()
+        up(BLOCKS[7], 0)
+        h_mul(BLOCKS[7], 0)
+        hm_quant(BLOCKS[4])
+        up(BLOCKS[7], 1)
+        h_mul(BLOCKS[7], 1)
+        h_turn(BLOCKS[6],"SS")
+        y_next(0,"V")
+        la_quant()
+        up(BLOCKS[7], 2)
+        h_mul(BLOCKS[7], 2)
+        y_next(0,"S")
+        up(BLOCKS[7], 3)
+        h_mul(BLOCKS[7], 3)
+        y_next(0,"S")
+        hf_quant(BLOCKS[6])
+        h_turn(BLOCKS[7], "SV")
+        y_next(0, "SV")
+        hf_quant(BLOCKS[7])
+        z_out(0, "S")
+        hm_quant(BLOCKS[6])
+        hm_quant(BLOCKS[5])
+        da_out(2, "V")
+        y_next(0, "V")
+        hm_quant(BLOCKS[7])
+        y_next(1, "SV")
+        da_out(3, "S")
+        z_out(1, "V")
+        y_next(1, "SVSVSV")

@@ -55,46 +55,30 @@ def tile_qlora_down_projection_s8_kernel(
         def load_x(g, s):
             nc.sync.dma_start(out=x_raw[g][:, s, :], in_=xv[g, :, s, :])
 
-        def load_w(G, c, f0, f1):
-            nc.sync.dma_start(out=w_raw[G, c][:, :, f0:f1], in_=wv[c, :, :, G * GF + f0 : G * GF + f1])
+        def load_w(G, c):
+            nc.sync.dma_start(out=w_raw[G, c][:], in_=wv[c, :, :, G * GF : (G + 1) * GF])
 
-        def load_gate(G, g):
-            nc.sync.dma_start(out=gate_sb[G, g][:], in_=gv[g, :, :, G * GF : (G + 1) * GF])
+        def load_gate(b):
+            G, g = b
+            nc.sync.dma_start(out=gate_sb[b][:], in_=gv[g, :, :, G * GF : (G + 1) * GF])
 
-        load_w(0, 0, 0, 512)
-        load_x(0, 0)
-        load_w(0, 1, 0, 512)
-        load_x(0, 1)
-        load_x(0, 2)
-        load_x(0, 3)
-        load_gate(0, 0)
-        for s in range(4):
-            load_x(1, s)
-        load_gate(0, 1)
-        load_w(1, 0, 0, 512)
-        load_w(1, 1, 0, 512)
-        load_gate(1, 0)
-        load_gate(1, 1)
-        load_w(2, 0, 0, 512)
-        load_w(2, 1, 0, 512)
-        load_gate(2, 0)
-        load_w(3, 0, 0, 512)
-        load_w(3, 1, 0, 512)
-        load_gate(3, 0)
-        nc.sync.dma_start(out=dz_raw[:], in_=dz.rearrange("(g p t) r -> p g (t r)", p=P, t=4))
-        for Q in range(4):
+        def load_dz():
+            nc.sync.dma_start(out=dz_raw[:], in_=dz.rearrange("(g p t) r -> p g (t r)", p=P, t=4))
+
+        def load_down():
+            for Q in range(4):
+                nc.sync.dma_start(
+                    out=dsc[32 * Q : 32 * Q + 4, :, :].bitcast(I32),
+                    in_=down_scales[:, 4 * Q : 4 * Q + 4, :].bitcast(I32).rearrange("g q w -> q g w"),
+                )
+            nc.sync.dma_start(out=words[:], in_=down_words.rearrange("g p w -> p g w"))
+
+        def load_lora():
+            nc.sync.dma_start(out=lbytes[:], in_=lora_a_bytes.rearrange("(g p t) r -> p g (t r)", p=P, t=4))
             nc.sync.dma_start(
-                out=dsc[32 * Q : 32 * Q + 4, :, :].bitcast(I32),
-                in_=down_scales[:, 4 * Q : 4 * Q + 4, :].bitcast(I32).rearrange("g q w -> q g w"),
+                out=lscale[:].rearrange("p (g t) -> p g t", t=4),
+                in_=lora_a_scale.rearrange("(g p t) o -> p g (t o)", p=P, t=4),
             )
-        nc.sync.dma_start(out=words[:], in_=down_words.rearrange("g p w -> p g w"))
-        load_gate(2, 1)
-        nc.sync.dma_start(out=lbytes[:], in_=lora_a_bytes.rearrange("(g p t) r -> p g (t r)", p=P, t=4))
-        nc.sync.dma_start(
-            out=lscale[:].rearrange("p (g t) -> p g t", t=4),
-            in_=lora_a_scale.rearrange("(g p t) o -> p g (t o)", p=P, t=4),
-        )
-        load_gate(3, 1)
 
         x_codes = {(g, s): kept("xc%d%d" % (g, s), [P, 2 * P], U32) for g in range(2) for s in range(4)}
         x_scales = {(g, s): kept("xs%d%d" % (g, s), [P, 2 * P], U8) for g in range(2) for s in range(4)}
@@ -117,12 +101,20 @@ def tile_qlora_down_projection_s8_kernel(
 
         xg = {}
 
-        def x_turn(g, s, engine):
+        x_bank = {}
+        h_bank = {}
+        out_bank = {}
+
+        def x_turn(g, s):
             bank = psum.tile([P, 4, P], F32, name="tr", bufs=2)
             xw = x_raw[g][:, s, :].bitcast(F32)
             for c in range(2):
                 for u in range(2):
                     nc.tensor.transpose(bank[:, 2 * c + u, :], xw[:, 256 * c + u : 256 * (c + 1) : 2], ident[:])
+            x_bank[g, s] = bank
+
+        def x_copy(g, s, engine):
+            bank = x_bank[g, s]
             t = work.tile([P, 2 * P * 4], BF16, name="xg", bufs=2, align_bytes=64)
             copy_on(
                 engine,
@@ -141,11 +133,11 @@ def tile_qlora_down_projection_s8_kernel(
                 wt = work.tile([P, GF * 4], BF16, name="wg", bufs=4, align_bytes=64)
                 wg[G, c] = wt
             t = wg[G, c][:, 1024 * half : 1024 * (half + 1)]
-            src = w_raw[G, c][:]
+            src = w_raw[G, c][:, :, 256 * half : 256 * (half + 1)]
             copy_on(
                 engine,
-                t.rearrange("p (t q j) -> p t q j", t=2, j=4),
-                src.rearrange("p j (q t) -> p t q j", t=4)[:, 2 * half : 2 * half + 2],
+                t.rearrange("p (f i j) -> p f j i", i=4, j=4),
+                src.rearrange("p j (f i) -> p f j i", i=4),
             )
 
         def w_quant(G, c, f0, f1):
@@ -156,96 +148,120 @@ def tile_qlora_down_projection_s8_kernel(
             )
 
         up_bank = {}
-        h_tile = {}
 
-        def up(b, i):
+        def up(b, s):
             G, g = b
-            bank = psum.tile([P, 4, P], F32, name="up", bufs=3)
-            fs = slice(128 * i, 128 * (i + 1))
-            for s in range(4):
-                for c in range(2):
-                    ks = slice(P * c, P * (c + 1))
-                    nc.tensor.matmul_mx(
-                        out=bank[:, s, :],
-                        lhsT=x_codes[g, s][:, ks].bitcast(FP8X4),
-                        lhsT_scale=x_scales[g, s][:, ks],
-                        rhs=w_codes[G, c][:, fs].bitcast(FP8X4),
-                        rhs_scale=w_scales[G, c][:, fs],
-                        start=(c == 0),
-                        stop=(c == 1),
-                    )
-            up_bank[b, i] = bank
+            bank = psum.tile([P, GF], F32, name="up", bufs=3)
+            for c in range(2):
+                ks = slice(P * c, P * (c + 1))
+                nc.tensor.matmul_mx(
+                    out=bank[:],
+                    lhsT=x_codes[g, s][:, ks].bitcast(FP8X4),
+                    lhsT_scale=x_scales[g, s][:, ks],
+                    rhs=w_codes[G, c][:].bitcast(FP8X4),
+                    rhs_scale=w_scales[G, c][:],
+                    start=(c == 0),
+                    stop=(c == 1),
+                )
+            up_bank[b, s] = bank
 
-        def h_mul(b, i):
-            if i == 0:
-                ht = work.tile([P, GF * 4], BF16, name="h", bufs=5, align_bytes=64)
-                h_tile[b] = ht
+        def h_mul(b, s):
             nc.vector.scalar_tensor_tensor(
-                out=h_tile[b][:].rearrange("p (t q s) -> p t q s", t=4, s=4)[:, i],
-                in0=gate_sb[b][:].rearrange("p s (q t) -> p t q s", t=4)[:, i],
+                out=gate_sb[b][:, s, :],
+                in0=gate_sb[b][:, s, :],
                 scalar=0.0,
-                in1=up_bank[b, i][:].rearrange("p s q -> p q s"),
+                in1=up_bank[b, s][:],
                 op0=ALU.max,
                 op1=ALU.mult,
             )
 
+        hm_tile = {}
+
+        def hm_mix(b, half, engine):
+            if half == 0:
+                hmt = work.tile([P, GF * 4], BF16, name="wg", bufs=4, align_bytes=64)
+                hm_tile[b] = hmt
+            copy_on(
+                engine,
+                hm_tile[b][:, 1024 * half : 1024 * (half + 1)].rearrange("p (f i s) -> p f s i", i=4, s=4),
+                gate_sb[b][:, :, 256 * half : 256 * (half + 1)].rearrange("p s (f i) -> p f s i", i=4),
+            )
+
         def hm_quant(b):
-            nc.vector.quantize_mx(out=hm_codes[b][:].bitcast(FP8X4), scales=hm_scales[b][:], in_=h_tile[b][:])
+            nc.vector.quantize_mx(out=hm_codes[b][:].bitcast(FP8X4), scales=hm_scales[b][:], in_=hm_tile[b][:])
 
         hf_tile = {}
 
-        def h_turn(b, engines):
-            hw = h_tile[b][:].bitcast(F32)
-            hft = work.tile([P, GM * 4], BF16, name="hf", bufs=2, align_bytes=64)
-            hf_tile[b] = hft
-            for u in range(2):
-                bank = psum.tile([P, 4, P], F32, name="tr", bufs=2)
-                for t in range(4):
-                    nc.tensor.transpose(bank[:, t, :], hw[:, 256 * t + u : 256 * (t + 1) : 2], ident[:])
-                copy_on(
-                    engines[u],
-                    hft[:].rearrange("p (u e q t) -> p u e q t", u=2, e=2, t=4)[:, u],
-                    bank[:].bitcast(BF16).rearrange("p t (q e) -> p e q t", e=2),
-                )
+        def h_turn(b, half):
+            bank = psum.tile([P, 4, P], F32, name="tr", bufs=2)
+            for k in range(2):
+                hw = gate_sb[b][:, 2 * half + k, :].bitcast(F32)
+                for u in range(2):
+                    nc.tensor.transpose(bank[:, 2 * k + u, :], hw[:, u : GF // 2 : 2], ident[:])
+            h_bank[b, half] = bank
 
-        def hf_quant(b):
-            nc.vector.quantize_mx(out=hf_codes[b][:].bitcast(FP8X4), scales=hf_scales[b][:], in_=hf_tile[b][:])
+        def h_copy(b, half, engine):
+            hft = work.tile([P, GM * 2], BF16, name="hf", bufs=4, align_bytes=64)
+            hf_tile[b, half] = hft
+            copy_on(
+                engine,
+                hft[:].bitcast(F32).rearrange("p (s q u) -> p s q u", s=2, u=2),
+                h_bank[b, half][:].rearrange("p (s u) q -> p s q u", u=2),
+            )
 
-        def dz_prep():
-            t = work.tile([P, 2 * R * 4], BF16, name="xg", bufs=2, align_bytes=64)
-            for g in range(2):
-                nc.scalar.copy(
-                    out=t[:, 512 * g : 512 * (g + 1)].rearrange("p (r t) -> p r t", t=4),
-                    in_=dz_raw[:, g, :].rearrange("p (t r) -> p r t", t=4),
-                )
-            nc.vector.quantize_mx(out=dz_codes[:].bitcast(FP8X4), scales=dz_scales[:], in_=t[:])
+        def hf_quant(b, half):
+            cols = slice(256 * half, 256 * (half + 1))
+            nc.vector.quantize_mx(
+                out=hf_codes[b][:, cols].bitcast(FP8X4), scales=hf_scales[b][:, cols], in_=hf_tile[b, half][:]
+            )
+
+        dzg = {}
+
+        def dz_mix(g, engine):
+            if g == 0:
+                dzt = work.tile([P, 2 * R * 4], BF16, name="xg", bufs=2, align_bytes=64)
+                dzg[0] = dzt
+            copy_on(
+                engine,
+                dzg[0][:, 512 * g : 512 * (g + 1)].rearrange("p (r t) -> p r t", t=4),
+                dz_raw[:, g, :].rearrange("p (t r) -> p r t", t=4),
+            )
+
+        def dz_quant():
+            nc.vector.quantize_mx(out=dz_codes[:].bitcast(FP8X4), scales=dz_scales[:], in_=dzg[0][:])
 
         lora = {}
 
-        def la_widen():
-            t = work.tile([P, 4, 4, R], BF16, name="wg", bufs=4, align_bytes=64)
-            for G in range(4):
-                for j in range(4):
-                    nc.scalar.activation(
-                        out=t[:, G, j, :],
-                        in_=lbytes[:, G, R * j : R * (j + 1)].bitcast(FP8),
-                        func=COPY,
-                        scale=lscale[:, 4 * G + j : 4 * G + j + 1],
-                    )
-            lora[0] = t
+        def la_widen(G):
+            if G == 0:
+                lt = work.tile([P, 4, 4, R], BF16, name="wg", bufs=4, align_bytes=64)
+                lora[0] = lt
+            for j in range(4):
+                nc.scalar.activation(
+                    out=lora[0][:, G, j, :],
+                    in_=lbytes[:, G, R * j : R * (j + 1)].bitcast(FP8),
+                    func=COPY,
+                    scale=lscale[:, 4 * G + j : 4 * G + j + 1],
+                )
+
+        def la_mix(half, engine):
+            if half == 0:
+                lm = work.tile([P, 4 * R * 4], BF16, name="wg", bufs=4, align_bytes=64)
+                lora[1] = lm
+            copy_on(
+                engine,
+                lora[1][:, 1024 * half : 1024 * (half + 1)].rearrange("p (g r j) -> p g r j", g=2, j=4),
+                lora[0][:, 2 * half : 2 * half + 2].rearrange("p g j r -> p g r j"),
+            )
 
         def la_quant():
-            t = work.tile([P, 4 * R * 4], BF16, name="wg", bufs=4, align_bytes=64)
-            nc.vector.tensor_copy(
-                out=t[:].rearrange("p (g r j) -> p g r j", g=4, j=4), in_=lora[0][:].rearrange("p g j r -> p g r j")
-            )
-            nc.vector.quantize_mx(out=la_codes[:].bitcast(FP8X4), scales=la_scales[:], in_=t[:])
+            nc.vector.quantize_mx(out=la_codes[:].bitcast(FP8X4), scales=la_scales[:], in_=lora[1][:])
 
         yv = y.rearrange("(g q s) n -> g s q n", q=P, s=4)
         zv = z.rearrange("(g q s) r -> g q s r", q=P, s=4)
-        dav = da.rearrange("(g q t) r -> g q t r", q=P, t=4)
+        dav = da.rearrange("(g t q) r -> g q t r", q=P, t=4)
 
-        def y_out(g, s, half, engine):
+        def y_mul(g, s, half):
             bank = psum.tile([P, 512], F32, name="acc", bufs=3)
             ns = slice(512 * half, 512 * (half + 1))
             for G in range(4):
@@ -258,11 +274,14 @@ def tile_qlora_down_projection_s8_kernel(
                     start=(G == 0),
                     stop=(G == 3),
                 )
-            t = work.tile([P, 512], F32, name="yo", bufs=5)
-            copy_on(engine, t[:], bank[:])
-            nc.sync.dma_start(out=yv[g, s, :, ns], in_=t[:])
+            out_bank["y", g, s, half] = bank
 
-        def z_out(g, engine):
+        def y_copy(g, s, half, engine):
+            t = work.tile([P, 512], F32, name="yo", bufs=5)
+            copy_on(engine, t[:], out_bank["y", g, s, half][:])
+            nc.sync.dma_start(out=yv[g, s, :, 512 * half : 512 * (half + 1)], in_=t[:])
+
+        def z_mul(g):
             bank = psum.tile([P, 4, R], F32, name="acc", bufs=3)
             for s in range(4):
                 for G in range(4):
@@ -275,11 +294,14 @@ def tile_qlora_down_projection_s8_kernel(
                         start=(G == 0),
                         stop=(G == 3),
                     )
+            out_bank["z", g] = bank
+
+        def z_copy(g, engine):
             t = work.tile([P, 4, R], F32, name="yo", bufs=5)
-            copy_on(engine, t[:], bank[:])
+            copy_on(engine, t[:], out_bank["z", g][:])
             nc.sync.dma_start(out=zv[g], in_=t[:])
 
-        def da_out(G, engine):
+        def da_mul(G):
             bank = psum.tile([P, 4, R], F32, name="acc", bufs=3)
             for t in range(4):
                 for g in range(2):
@@ -292,158 +314,276 @@ def tile_qlora_down_projection_s8_kernel(
                         start=(g == 0),
                         stop=(g == 1),
                     )
+            out_bank["da", G] = bank
+
+        def da_copy(G, engine):
             t = work.tile([P, 4, R], F32, name="yo", bufs=5)
-            copy_on(engine, t[:], bank[:])
+            copy_on(engine, t[:], out_bank["da", G][:])
             nc.sync.dma_start(out=dav[G], in_=t[:])
 
-        def y_next(g, engines):
-            for e in engines:
-                s, half = y_todo[g].pop(0)
-                y_out(g, s, half, e)
-
-        y_todo = {g: [(s, half) for s in range(4) for half in range(2)] for g in range(2)}
-        w_mix(0, 0, 0, "V")
-        w_mix(0, 0, 1, "S")
-        x_turn(0, 0, "S")
-        w_quant(0, 0, 0, 512)
-        w_mix(0, 1, 0, "V")
-        w_mix(0, 1, 1, "S")
-        x_quant(0, 0)
-        x_turn(0, 1, "V")
-        w_quant(0, 1, 0, 512)
-        x_turn(0, 2, "S")
-        x_quant(0, 1)
-        x_turn(0, 3, "S")
-        x_quant(0, 2)
-        x_quant(0, 3)
-        x_turn(1, 0, "S")
-        up(BLOCKS[0], 0)
-        h_mul(BLOCKS[0], 0)
-        x_turn(1,1,"S")
-        x_quant(1,0)
-        up(BLOCKS[0], 1)
-        h_mul(BLOCKS[0], 1)
-        x_turn(1,2,"S")
-        x_quant(1,1)
-        up(BLOCKS[0], 2)
-        h_mul(BLOCKS[0], 2)
-        x_turn(1,3,"S")
-        x_quant(1,2)
-        up(BLOCKS[0], 3)
-        h_mul(BLOCKS[0], 3)
+        ctx.enter_context(tc.manual_schedule())
+        load_x(1,3)
+        x_turn(1,3)
+        load_w(0,0)
+        x_copy(1,3,"S")
+        w_mix(0,0,0,"V")
+        load_w(0,1)
+        load_x(0,0)
+        w_mix(0,1,0,"V")
+        x_turn(0,0)
+        load_x(0,1)
+        w_mix(0,0,1,"S")
+        load_x(1,1)
+        w_mix(0,1,1,"V")
         x_quant(1,3)
-        w_mix(1,0,0,"S")
-        w_mix(1,0,1,"V")
-        up(BLOCKS[1], 0)
-        h_mul(BLOCKS[1], 0)
+        x_turn(0,1)
+        load_x(1,2)
+        load_x(1,0)
+        x_copy(0,0,"S")
+        load_w(1,1)
+        load_gate(BLOCKS[0])
+        x_turn(1,1)
+        x_quant(0,0)
+        w_quant(0,0,0,512)
+        x_copy(0,1,"S")
+        load_w(1,0)
+        x_copy(1,1,"S")
+        x_quant(0,1)
+        w_quant(0,1,0,512)
+        x_turn(1,2)
+        x_quant(1,1)
+        load_gate(BLOCKS[1])
         w_mix(1,1,0,"V")
-        w_quant(1,0,0,512)
-        up(BLOCKS[1], 1)
-        h_mul(BLOCKS[1], 1)
-        h_turn(BLOCKS[0],"SS")
+        x_turn(1,0)
+        up(BLOCKS[0],1)
+        x_copy(1,2,"S")
+        up(BLOCKS[0],0)
+        x_quant(1,2)
+        up(BLOCKS[1],1)
+        h_mul(BLOCKS[0],1)
+        x_copy(1,0,"S")
         w_mix(1,1,1,"S")
-        up(BLOCKS[1], 2)
-        h_mul(BLOCKS[1], 2)
+        h_mul(BLOCKS[0],0)
+        x_quant(1,0)
+        up(BLOCKS[1],3)
         w_quant(1,1,0,512)
-        up(BLOCKS[1], 3)
-        h_mul(BLOCKS[1], 3)
-        up(BLOCKS[2], 0)
-        h_mul(BLOCKS[2], 0)
-        hf_quant(BLOCKS[0])
-        w_mix(2,0,0,"S")
-        up(BLOCKS[2], 1)
-        h_mul(BLOCKS[2], 1)
-        h_turn(BLOCKS[1],"SS")
-        w_mix(2,1,0,"V")
-        up(BLOCKS[2], 2)
-        h_mul(BLOCKS[2], 2)
-        w_mix(2,0,1,"S")
-        up(BLOCKS[2], 3)
-        h_mul(BLOCKS[2], 3)
-        w_quant(2,0,0,512)
-        up(BLOCKS[3], 0)
-        h_mul(BLOCKS[3], 0)
-        hf_quant(BLOCKS[1])
+        w_mix(1,0,0,"S")
+        load_x(0,2)
+        h_mul(BLOCKS[1],1)
+        h_turn(BLOCKS[0],0)
+        h_mul(BLOCKS[1],3)
+        w_mix(1,0,1,"S")
+        up(BLOCKS[1],2)
+        h_copy(BLOCKS[0],0,"S")
+        h_mul(BLOCKS[1],2)
+        up(BLOCKS[1],0)
+        x_turn(0,2)
+        load_x(0,3)
+        x_turn(0,3)
+        x_copy(0,2,"S")
+        w_quant(1,0,0,512)
+        load_w(2,1)
+        h_mul(BLOCKS[1],0)
+        x_quant(0,2)
+        up(BLOCKS[3],2)
+        hf_quant(BLOCKS[0],0)
+        up(BLOCKS[3],1)
+        load_gate(BLOCKS[3])
+        load_gate(BLOCKS[2])
+        w_mix(2,1,0,"S")
+        h_mul(BLOCKS[3],2)
+        up(BLOCKS[3],0)
+        h_mul(BLOCKS[3],1)
+        h_mul(BLOCKS[3],0)
+        up(BLOCKS[2],1)
+        h_mul(BLOCKS[2],1)
+        up(BLOCKS[2],0)
         w_mix(2,1,1,"S")
-        up(BLOCKS[3], 1)
-        h_mul(BLOCKS[3], 1)
-        h_turn(BLOCKS[2],"SS")
-        w_quant(2,1,0,512)
-        up(BLOCKS[3], 2)
-        h_mul(BLOCKS[3], 2)
+        up(BLOCKS[2],2)
+        load_w(3,0)
+        x_copy(0,3,"S")
+        h_turn(BLOCKS[1],0)
         w_mix(3,0,0,"S")
-        w_mix(3,1,0,"V")
-        up(BLOCKS[3], 3)
-        h_mul(BLOCKS[3], 3)
+        load_w(2,0)
+        h_mul(BLOCKS[2],0)
+        up(BLOCKS[3],3)
+        h_copy(BLOCKS[1],0,"S")
+        w_mix(2,0,0,"S")
+        load_gate(BLOCKS[4])
+        up(BLOCKS[0],2)
+        x_quant(0,3)
+        h_turn(BLOCKS[1],1)
+        w_quant(2,1,0,512)
+        h_copy(BLOCKS[1],1,"S")
+        w_mix(2,0,1,"V")
+        h_turn(BLOCKS[3],0)
+        h_mul(BLOCKS[2],2)
+        up(BLOCKS[0],3)
+        h_mul(BLOCKS[3],3)
+        w_quant(2,0,0,512)
+        h_mul(BLOCKS[0],2)
+        up(BLOCKS[4],3)
+        h_copy(BLOCKS[3],0,"S")
+        load_w(3,1)
+        w_mix(3,1,0,"S")
+        h_mul(BLOCKS[0],3)
+        up(BLOCKS[4],0)
+        hf_quant(BLOCKS[1],0)
+        h_mul(BLOCKS[4],0)
+        up(BLOCKS[2],3)
+        load_gate(BLOCKS[7])
         w_mix(3,0,1,"S")
-        up(BLOCKS[4], 0)
-        h_mul(BLOCKS[4], 0)
-        hf_quant(BLOCKS[2])
-        w_quant(3,0,0,512)
-        up(BLOCKS[4], 1)
-        h_mul(BLOCKS[4], 1)
-        h_turn(BLOCKS[3],"SS")
+        h_mul(BLOCKS[4],3)
+        hf_quant(BLOCKS[3],0)
+        h_turn(BLOCKS[0],1)
+        h_mul(BLOCKS[2],3)
+        h_turn(BLOCKS[2],0)
+        up(BLOCKS[4],1)
+        h_copy(BLOCKS[0],1,"S")
+        up(BLOCKS[6],1)
         w_mix(3,1,1,"S")
-        up(BLOCKS[4], 2)
-        h_mul(BLOCKS[4], 2)
+        load_gate(BLOCKS[5])
+        load_gate(BLOCKS[6])
+        w_quant(3,0,0,512)
+        up(BLOCKS[4],2)
+        h_copy(BLOCKS[2],0,"S")
+        h_mul(BLOCKS[4],1)
+        hf_quant(BLOCKS[1],1)
         w_quant(3,1,0,512)
-        up(BLOCKS[4], 3)
-        h_mul(BLOCKS[4], 3)
-        hm_quant(BLOCKS[0])
-        up(BLOCKS[5], 0)
-        h_mul(BLOCKS[5], 0)
-        hf_quant(BLOCKS[3])
-        up(BLOCKS[5], 1)
-        h_mul(BLOCKS[5], 1)
-        h_turn(BLOCKS[4],"SS")
-        up(BLOCKS[5], 2)
-        h_mul(BLOCKS[5], 2)
+        h_turn(BLOCKS[2],1)
+        h_mul(BLOCKS[6],1)
+        load_down()
+        h_turn(BLOCKS[4],0)
+        up(BLOCKS[5],1)
+        hm_mix(BLOCKS[1],0,"S")
+        h_mul(BLOCKS[4],2)
+        up(BLOCKS[7],1)
+        up(BLOCKS[5],0)
+        h_mul(BLOCKS[5],1)
+        up(BLOCKS[5],3)
+        h_mul(BLOCKS[7],1)
+        hm_mix(BLOCKS[3],0,"S")
+        h_copy(BLOCKS[2],1,"S")
+        h_mul(BLOCKS[5],0)
+        up(BLOCKS[5],2)
+        hf_quant(BLOCKS[0],1)
+        h_mul(BLOCKS[5],3)
+        hf_quant(BLOCKS[2],0)
+        up(BLOCKS[7],0)
+        h_mul(BLOCKS[5],2)
+        h_turn(BLOCKS[4],1)
+        h_copy(BLOCKS[4],0,"S")
+        h_mul(BLOCKS[7],0)
+        hm_mix(BLOCKS[3],1,"S")
+        load_lora()
+        h_copy(BLOCKS[4],1,"S")
+        h_turn(BLOCKS[5],0)
+        hf_quant(BLOCKS[4],0)
+        h_copy(BLOCKS[5],0,"V")
+        up(BLOCKS[7],3)
+        h_mul(BLOCKS[7],3)
+        hf_quant(BLOCKS[5],0)
+        la_widen(0)
+        up(BLOCKS[7],2)
+        up(BLOCKS[6],3)
+        h_mul(BLOCKS[7],2)
+        h_turn(BLOCKS[7],0)
+        hf_quant(BLOCKS[2],1)
+        h_mul(BLOCKS[6],3)
+        h_turn(BLOCKS[5],1)
+        hm_mix(BLOCKS[1],1,"S")
+        up(BLOCKS[6],0)
+        h_copy(BLOCKS[7],0,"V")
+        up(BLOCKS[6],2)
+        y_mul(0,0,1)
+        h_copy(BLOCKS[5],1,"S")
+        y_mul(0,1,1)
+        la_widen(3)
+        load_dz()
+        h_turn(BLOCKS[7],1)
+        h_mul(BLOCKS[6],2)
+        hf_quant(BLOCKS[4],1)
+        h_mul(BLOCKS[6],0)
+        h_turn(BLOCKS[6],0)
+        y_copy(0,0,1,"S")
         hm_quant(BLOCKS[1])
-        dz_prep()
-        up(BLOCKS[5], 3)
-        h_mul(BLOCKS[5], 3)
-        hm_quant(BLOCKS[2])
-        up(BLOCKS[6], 0)
-        h_mul(BLOCKS[6], 0)
-        hf_quant(BLOCKS[4])
-        up(BLOCKS[6], 1)
-        h_mul(BLOCKS[6], 1)
-        h_turn(BLOCKS[5],"SV")
-        da_out(0,"S")
-        up(BLOCKS[6], 2)
-        h_mul(BLOCKS[6], 2)
+        hf_quant(BLOCKS[5],1)
+        y_copy(0,1,1,"V")
+        la_widen(2)
+        dz_mix(0,"V")
+        hf_quant(BLOCKS[7],0)
+        la_widen(1)
+        y_mul(0,2,0)
+        h_copy(BLOCKS[6],0,"S")
+        la_mix(0,"S")
+        hm_mix(BLOCKS[0],0,"S")
+        y_mul(0,0,0)
+        h_copy(BLOCKS[7],1,"V")
+        h_turn(BLOCKS[6],1)
+        la_mix(1,"V")
+        h_turn(BLOCKS[3],1)
+        y_copy(0,2,0,"V")
         hm_quant(BLOCKS[3])
-        up(BLOCKS[6], 3)
-        h_mul(BLOCKS[6], 3)
-        hf_quant(BLOCKS[5])
-        da_out(1,"S")
-        y_next(0,"VS")
-        la_widen()
-        up(BLOCKS[7], 0)
-        h_mul(BLOCKS[7], 0)
-        hm_quant(BLOCKS[4])
-        up(BLOCKS[7], 1)
-        h_mul(BLOCKS[7], 1)
-        h_turn(BLOCKS[6],"SS")
-        y_next(0,"V")
+        y_mul(0,3,0)
+        hf_quant(BLOCKS[6],0)
+        y_copy(0,0,0,"V")
+        y_mul(1,0,1)
+        h_copy(BLOCKS[3],1,"S")
+        y_copy(0,3,0,"S")
+        hm_mix(BLOCKS[2],0,"V")
+        hf_quant(BLOCKS[7],1)
+        h_copy(BLOCKS[6],1,"S")
+        hf_quant(BLOCKS[3],1)
+        y_copy(1,0,1,"V")
+        hm_mix(BLOCKS[2],1,"S")
+        y_mul(0,3,1)
+        y_mul(1,1,1)
+        y_copy(1,1,1,"S")
+        y_mul(1,1,0)
+        y_copy(0,3,1,"V")
+        hf_quant(BLOCKS[6],1)
+        hm_quant(BLOCKS[2])
+        y_mul(0,1,0)
+        hm_mix(BLOCKS[0],1,"S")
+        dz_mix(1,"V")
+        y_copy(1,1,0,"V")
+        y_copy(0,1,0,"S")
+        y_mul(1,3,0)
+        hm_mix(BLOCKS[7],0,"V")
+        hm_quant(BLOCKS[0])
+        dz_quant()
+        y_mul(1,2,0)
         la_quant()
-        up(BLOCKS[7], 2)
-        h_mul(BLOCKS[7], 2)
-        y_next(0,"S")
-        up(BLOCKS[7], 3)
-        h_mul(BLOCKS[7], 3)
-        y_next(0,"S")
-        hf_quant(BLOCKS[6])
-        h_turn(BLOCKS[7], "SV")
-        y_next(0, "SV")
-        hf_quant(BLOCKS[7])
-        z_out(0, "S")
-        hm_quant(BLOCKS[6])
-        hm_quant(BLOCKS[5])
-        da_out(2, "V")
-        y_next(0, "V")
+        hm_mix(BLOCKS[6],0,"V")
+        hm_mix(BLOCKS[4],0,"V")
+        y_copy(1,3,0,"S")
+        hm_mix(BLOCKS[5],0,"V")
+        z_mul(0)
+        y_copy(1,2,0,"S")
+        da_mul(1)
+        y_mul(1,2,1)
+        hm_mix(BLOCKS[7],1,"S")
+        z_copy(0,"V")
+        hm_mix(BLOCKS[5],1,"V")
+        z_mul(1)
+        da_copy(1,"S")
+        hm_mix(BLOCKS[4],1,"S")
         hm_quant(BLOCKS[7])
-        y_next(1, "SV")
-        da_out(3, "S")
-        z_out(1, "V")
-        y_next(1, "SVSVSV")
+        y_copy(1,2,1,"S")
+        z_copy(1,"S")
+        y_mul(1,3,1)
+        hm_mix(BLOCKS[6],1,"V")
+        hm_quant(BLOCKS[4])
+        y_copy(1,3,1,"V")
+        y_mul(1,0,0)
+        hm_quant(BLOCKS[5])
+        hm_quant(BLOCKS[6])
+        da_mul(0)
+        y_copy(1,0,0,"S")
+        da_mul(3)
+        da_mul(2)
+        da_copy(0,"S")
+        da_copy(3,"V")
+        da_copy(2,"V")
+        y_mul(0,2,1)
+        y_copy(0,2,1,"S")

from contextlib import ExitStack

import concourse.mybir as mybir
from concourse.masks import make_identity

M, K, F, N, R = 1024, 1024, 2048, 1024, 128
FLOPS = 2 * M * K * F + 2 * M * F * N + 4 * M * F * R

F32 = mybir.dt.float32
BF16 = mybir.dt.bfloat16
I32 = mybir.dt.int32
U32 = mybir.dt.uint32
U8 = mybir.dt.uint8
FP8 = mybir.dt.float8_e4m3fn
FP8X4 = mybir.dt.float8_e4m3fn_x4
FP4X4 = mybir.dt.float4_e2m1fn_x4
ALU = mybir.AluOpType
COPY = mybir.ActivationFunctionType.Copy

P = 128
GM = 512
GF = 512
BLOCKS = [(0, 0), (0, 1), (1, 0), (1, 1), (2, 0), (3, 0), (2, 1), (3, 1)]


def tile_qlora_down_projection_s8_kernel(
    tc, x, w_up, gate, down_words, down_scales, lora_a_bytes, lora_a_scale, dz, y, z, da
):
    nc = tc.nc
    with ExitStack() as ctx:
        keep = ctx.enter_context(tc.tile_pool(name="keep", bufs=1))
        work = ctx.enter_context(tc.tile_pool(name="work", bufs=2))
        psum = ctx.enter_context(tc.psum_pool(name="psum", bufs=2))

        def kept(name, shape, dtype):
            return keep.tile(shape, dtype, name=name, align_bytes=64)

        ident = kept("ident", [P, P], F32)
        make_identity(nc, ident[:])
        dsc = kept("dsc", [P, 4, N], U8)
        nc.gpsimd.memset(dsc[:].rearrange("p g n -> p (g n)").bitcast(I32), 0)

        x_raw = [kept("x_raw%d" % g, [P, 4, K], BF16) for g in range(2)]
        w_raw = {(G, c): kept("w_raw%d%d" % (G, c), [P, 4, GF], BF16) for G in range(4) for c in range(2)}
        gate_sb = {b: kept("gate%d%d" % b, [P, 4, GF], BF16) for b in BLOCKS}
        words = kept("words", [P, 4, 2 * N], U8)
        lbytes = kept("lbytes", [P, 4, 4 * R], U8)
        lscale = kept("lscale", [P, 16], F32)
        dz_raw = kept("dz_raw", [P, 2, 4 * R], BF16)

        xv = x.rearrange("(g p s) k -> g p s k", p=P, s=4)
        wv = w_up.rearrange("(c p j) f -> c p j f", p=P, j=4)
        gv = gate.rearrange("(g p s) f -> g p s f", p=P, s=4)

        def load_x(g, s):
            nc.sync.dma_start(out=x_raw[g][:, s, :], in_=xv[g, :, s, :])

        def load_w(G, c):
            nc.sync.dma_start(out=w_raw[G, c][:], in_=wv[c, :, :, G * GF : (G + 1) * GF])

        def load_gate(b):
            G, g = b
            nc.sync.dma_start(out=gate_sb[b][:], in_=gv[g, :, :, G * GF : (G + 1) * GF])

        def load_dz():
            nc.sync.dma_start(out=dz_raw[:], in_=dz.rearrange("(g p t) r -> p g (t r)", p=P, t=4))

        def load_down():
            for Q in range(4):
                nc.sync.dma_start(
                    out=dsc[32 * Q : 32 * Q + 4, :, :].bitcast(I32),
                    in_=down_scales[:, 4 * Q : 4 * Q + 4, :].bitcast(I32).rearrange("g q w -> q g w"),
                )
            nc.sync.dma_start(out=words[:], in_=down_words.rearrange("g p w -> p g w"))

        def load_lora():
            nc.sync.dma_start(out=lbytes[:], in_=lora_a_bytes.rearrange("(g p t) r -> p g (t r)", p=P, t=4))
            nc.sync.dma_start(
                out=lscale[:].rearrange("p (g t) -> p g t", t=4),
                in_=lora_a_scale.rearrange("(g p t) o -> p g (t o)", p=P, t=4),
            )

        x_codes = {(g, s): kept("xc%d%d" % (g, s), [P, 2 * P], U32) for g in range(2) for s in range(4)}
        x_scales = {(g, s): kept("xs%d%d" % (g, s), [P, 2 * P], U8) for g in range(2) for s in range(4)}
        w_codes = {(G, c): kept("wc%d%d" % (G, c), [P, GF], U32) for G in range(4) for c in range(2)}
        w_scales = {(G, c): kept("ws%d%d" % (G, c), [P, GF], U8) for G in range(4) for c in range(2)}
        hm_codes = {b: kept("hmc%d%d" % b, [P, GF], U32) for b in BLOCKS}
        hm_scales = {b: kept("hms%d%d" % b, [P, GF], U8) for b in BLOCKS}
        hf_codes = {b: kept("hfc%d%d" % b, [P, GM], U32) for b in BLOCKS}
        hf_scales = {b: kept("hfs%d%d" % b, [P, GM], U8) for b in BLOCKS}
        dz_codes = kept("dzc", [P, 2 * R], U32)
        dz_scales = kept("dzs", [P, 2 * R], U8)
        la_codes = kept("lac", [P, 4 * R], U32)
        la_scales = kept("las", [P, 4 * R], U8)

        def copy_on(engine, out, in_):
            if engine == "V":
                nc.vector.tensor_copy(out=out, in_=in_)
            else:
                nc.scalar.copy(out=out, in_=in_)

        xg = {}

        x_bank = {}
        h_bank = {}
        out_bank = {}

        def x_turn(g, s):
            bank = psum.tile([P, 4, P], F32, name="tr", bufs=2)
            xw = x_raw[g][:, s, :].bitcast(F32)
            for c in range(2):
                for u in range(2):
                    nc.tensor.transpose(bank[:, 2 * c + u, :], xw[:, 256 * c + u : 256 * (c + 1) : 2], ident[:])
            x_bank[g, s] = bank

        def x_copy(g, s, engine):
            bank = x_bank[g, s]
            t = work.tile([P, 2 * P * 4], BF16, name="xg", bufs=2, align_bytes=64)
            copy_on(
                engine,
                t[:].bitcast(F32).rearrange("p (c q u) -> p c q u", c=2, u=2),
                bank[:].rearrange("p (c u) q -> p c q u", c=2),
            )
            xg[g, s] = t

        def x_quant(g, s):
            nc.vector.quantize_mx(out=x_codes[g, s][:].bitcast(FP8X4), scales=x_scales[g, s][:], in_=xg[g, s][:])

        wg = {}

        def w_mix(G, c, half, engine):
            if half == 0:
                wt = work.tile([P, GF * 4], BF16, name="wg", bufs=4, align_bytes=64)
                wg[G, c] = wt
            t = wg[G, c][:, 1024 * half : 1024 * (half + 1)]
            src = w_raw[G, c][:, :, 256 * half : 256 * (half + 1)]
            copy_on(
                engine,
                t.rearrange("p (f i j) -> p f j i", i=4, j=4),
                src.rearrange("p j (f i) -> p f j i", i=4),
            )

        def w_quant(G, c, f0, f1):
            nc.vector.quantize_mx(
                out=w_codes[G, c][:, f0:f1].bitcast(FP8X4),
                scales=w_scales[G, c][:, f0:f1],
                in_=wg[G, c][:, 4 * f0 : 4 * f1],
            )

        up_bank = {}

        def up(b, s):
            G, g = b
            bank = psum.tile([P, GF], F32, name="up", bufs=3)
            for c in range(2):
                ks = slice(P * c, P * (c + 1))
                nc.tensor.matmul_mx(
                    out=bank[:],
                    lhsT=x_codes[g, s][:, ks].bitcast(FP8X4),
                    lhsT_scale=x_scales[g, s][:, ks],
                    rhs=w_codes[G, c][:].bitcast(FP8X4),
                    rhs_scale=w_scales[G, c][:],
                    start=(c == 0),
                    stop=(c == 1),
                )
            up_bank[b, s] = bank

        def h_mul(b, s):
            nc.vector.scalar_tensor_tensor(
                out=gate_sb[b][:, s, :],
                in0=gate_sb[b][:, s, :],
                scalar=0.0,
                in1=up_bank[b, s][:],
                op0=ALU.max,
                op1=ALU.mult,
            )

        hm_tile = {}

        def hm_mix(b, half, engine):
            if half == 0:
                hmt = work.tile([P, GF * 4], BF16, name="wg", bufs=4, align_bytes=64)
                hm_tile[b] = hmt
            copy_on(
                engine,
                hm_tile[b][:, 1024 * half : 1024 * (half + 1)].rearrange("p (f i s) -> p f s i", i=4, s=4),
                gate_sb[b][:, :, 256 * half : 256 * (half + 1)].rearrange("p s (f i) -> p f s i", i=4),
            )

        def hm_quant(b):
            nc.vector.quantize_mx(out=hm_codes[b][:].bitcast(FP8X4), scales=hm_scales[b][:], in_=hm_tile[b][:])

        hf_tile = {}

        def h_turn(b, half):
            bank = psum.tile([P, 4, P], F32, name="tr", bufs=2)
            for k in range(2):
                hw = gate_sb[b][:, 2 * half + k, :].bitcast(F32)
                for u in range(2):
                    nc.tensor.transpose(bank[:, 2 * k + u, :], hw[:, u : GF // 2 : 2], ident[:])
            h_bank[b, half] = bank

        def h_copy(b, half, engine):
            hft = work.tile([P, GM * 2], BF16, name="hf", bufs=4, align_bytes=64)
            hf_tile[b, half] = hft
            copy_on(
                engine,
                hft[:].bitcast(F32).rearrange("p (s q u) -> p s q u", s=2, u=2),
                h_bank[b, half][:].rearrange("p (s u) q -> p s q u", u=2),
            )

        def hf_quant(b, half):
            cols = slice(256 * half, 256 * (half + 1))
            nc.vector.quantize_mx(
                out=hf_codes[b][:, cols].bitcast(FP8X4), scales=hf_scales[b][:, cols], in_=hf_tile[b, half][:]
            )

        dzg = {}

        def dz_mix(g, engine):
            if g == 0:
                dzt = work.tile([P, 2 * R * 4], BF16, name="xg", bufs=2, align_bytes=64)
                dzg[0] = dzt
            copy_on(
                engine,
                dzg[0][:, 512 * g : 512 * (g + 1)].rearrange("p (r t) -> p r t", t=4),
                dz_raw[:, g, :].rearrange("p (t r) -> p r t", t=4),
            )

        def dz_quant():
            nc.vector.quantize_mx(out=dz_codes[:].bitcast(FP8X4), scales=dz_scales[:], in_=dzg[0][:])

        lora = {}

        def la_widen(G):
            if G == 0:
                lt = work.tile([P, 4, 4, R], BF16, name="wg", bufs=4, align_bytes=64)
                lora[0] = lt
            for j in range(4):
                nc.scalar.activation(
                    out=lora[0][:, G, j, :],
                    in_=lbytes[:, G, R * j : R * (j + 1)].bitcast(FP8),
                    func=COPY,
                    scale=lscale[:, 4 * G + j : 4 * G + j + 1],
                )

        def la_mix(half, engine):
            if half == 0:
                lm = work.tile([P, 4 * R * 4], BF16, name="wg", bufs=4, align_bytes=64)
                lora[1] = lm
            copy_on(
                engine,
                lora[1][:, 1024 * half : 1024 * (half + 1)].rearrange("p (g r j) -> p g r j", g=2, j=4),
                lora[0][:, 2 * half : 2 * half + 2].rearrange("p g j r -> p g r j"),
            )

        def la_quant():
            nc.vector.quantize_mx(out=la_codes[:].bitcast(FP8X4), scales=la_scales[:], in_=lora[1][:])

        yv = y.rearrange("(g q s) n -> g s q n", q=P, s=4)
        zv = z.rearrange("(g q s) r -> g q s r", q=P, s=4)
        dav = da.rearrange("(g t q) r -> g q t r", q=P, t=4)

        def y_mul(g, s, half):
            bank = psum.tile([P, 512], F32, name="acc", bufs=3)
            ns = slice(512 * half, 512 * (half + 1))
            for G in range(4):
                nc.tensor.matmul_mx(
                    out=bank[:],
                    lhsT=hf_codes[G, g][:, P * s : P * (s + 1)].bitcast(FP8X4),
                    lhsT_scale=hf_scales[G, g][:, P * s : P * (s + 1)],
                    rhs=words[:, G, 1024 * half : 1024 * (half + 1)].bitcast(FP4X4),
                    rhs_scale=dsc[:, G, ns],
                    start=(G == 0),
                    stop=(G == 3),
                )
            out_bank["y", g, s, half] = bank

        def y_copy(g, s, half, engine):
            t = work.tile([P, 512], F32, name="yo", bufs=5)
            copy_on(engine, t[:], out_bank["y", g, s, half][:])
            nc.sync.dma_start(out=yv[g, s, :, 512 * half : 512 * (half + 1)], in_=t[:])

        def z_mul(g):
            bank = psum.tile([P, 4, R], F32, name="acc", bufs=3)
            for s in range(4):
                for G in range(4):
                    nc.tensor.matmul_mx(
                        out=bank[:, s, :],
                        lhsT=hf_codes[G, g][:, P * s : P * (s + 1)].bitcast(FP8X4),
                        lhsT_scale=hf_scales[G, g][:, P * s : P * (s + 1)],
                        rhs=la_codes[:, R * G : R * (G + 1)].bitcast(FP8X4),
                        rhs_scale=la_scales[:, R * G : R * (G + 1)],
                        start=(G == 0),
                        stop=(G == 3),
                    )
            out_bank["z", g] = bank

        def z_copy(g, engine):
            t = work.tile([P, 4, R], F32, name="yo", bufs=5)
            copy_on(engine, t[:], out_bank["z", g][:])
            nc.sync.dma_start(out=zv[g], in_=t[:])

        def da_mul(G):
            bank = psum.tile([P, 4, R], F32, name="acc", bufs=3)
            for t in range(4):
                for g in range(2):
                    nc.tensor.matmul_mx(
                        out=bank[:, t, :],
                        lhsT=hm_codes[G, g][:, P * t : P * (t + 1)].bitcast(FP8X4),
                        lhsT_scale=hm_scales[G, g][:, P * t : P * (t + 1)],
                        rhs=dz_codes[:, R * g : R * (g + 1)].bitcast(FP8X4),
                        rhs_scale=dz_scales[:, R * g : R * (g + 1)],
                        start=(g == 0),
                        stop=(g == 1),
                    )
            out_bank["da", G] = bank

        def da_copy(G, engine):
            t = work.tile([P, 4, R], F32, name="yo", bufs=5)
            copy_on(engine, t[:], out_bank["da", G][:])
            nc.sync.dma_start(out=dav[G], in_=t[:])

        ctx.enter_context(tc.manual_schedule())
        load_x(1,3)
        x_turn(1,3)
        load_w(0,0)
        x_copy(1,3,"S")
        w_mix(0,0,0,"V")
        load_w(0,1)
        load_x(0,0)
        w_mix(0,1,0,"V")
        x_turn(0,0)
        load_x(0,1)
        w_mix(0,0,1,"S")
        load_x(1,1)
        w_mix(0,1,1,"V")
        x_quant(1,3)
        x_turn(0,1)
        load_x(1,2)
        load_x(1,0)
        x_copy(0,0,"S")
        load_w(1,1)
        load_gate(BLOCKS[0])
        x_turn(1,1)
        x_quant(0,0)
        w_quant(0,0,0,512)
        x_copy(0,1,"S")
        load_w(1,0)
        x_copy(1,1,"S")
        x_quant(0,1)
        w_quant(0,1,0,512)
        x_turn(1,2)
        x_quant(1,1)
        load_gate(BLOCKS[1])
        w_mix(1,1,0,"V")
        x_turn(1,0)
        up(BLOCKS[0],1)
        x_copy(1,2,"S")
        up(BLOCKS[0],0)
        x_quant(1,2)
        up(BLOCKS[1],1)
        h_mul(BLOCKS[0],1)
        x_copy(1,0,"S")
        w_mix(1,1,1,"S")
        h_mul(BLOCKS[0],0)
        x_quant(1,0)
        up(BLOCKS[1],3)
        w_quant(1,1,0,512)
        w_mix(1,0,0,"S")
        load_x(0,2)
        h_mul(BLOCKS[1],1)
        h_turn(BLOCKS[0],0)
        h_mul(BLOCKS[1],3)
        w_mix(1,0,1,"S")
        up(BLOCKS[1],2)
        h_copy(BLOCKS[0],0,"S")
        h_mul(BLOCKS[1],2)
        up(BLOCKS[1],0)
        x_turn(0,2)
        load_x(0,3)
        x_turn(0,3)
        x_copy(0,2,"S")
        w_quant(1,0,0,512)
        load_w(2,1)
        h_mul(BLOCKS[1],0)
        x_quant(0,2)
        up(BLOCKS[3],2)
        hf_quant(BLOCKS[0],0)
        up(BLOCKS[3],1)
        load_gate(BLOCKS[3])
        load_gate(BLOCKS[2])
        w_mix(2,1,0,"S")
        h_mul(BLOCKS[3],2)
        up(BLOCKS[3],0)
        h_mul(BLOCKS[3],1)
        h_mul(BLOCKS[3],0)
        up(BLOCKS[2],1)
        h_mul(BLOCKS[2],1)
        up(BLOCKS[2],0)
        w_mix(2,1,1,"S")
        up(BLOCKS[2],2)
        load_w(3,0)
        x_copy(0,3,"S")
        h_turn(BLOCKS[1],0)
        w_mix(3,0,0,"S")
        load_w(2,0)
        h_mul(BLOCKS[2],0)
        up(BLOCKS[3],3)
        h_copy(BLOCKS[1],0,"S")
        w_mix(2,0,0,"S")
        load_gate(BLOCKS[4])
        up(BLOCKS[0],2)
        x_quant(0,3)
        h_turn(BLOCKS[1],1)
        w_quant(2,1,0,512)
        h_copy(BLOCKS[1],1,"S")
        w_mix(2,0,1,"V")
        h_turn(BLOCKS[3],0)
        h_mul(BLOCKS[2],2)
        up(BLOCKS[0],3)
        h_mul(BLOCKS[3],3)
        w_quant(2,0,0,512)
        h_mul(BLOCKS[0],2)
        up(BLOCKS[4],3)
        h_copy(BLOCKS[3],0,"S")
        load_w(3,1)
        w_mix(3,1,0,"S")
        h_mul(BLOCKS[0],3)
        up(BLOCKS[4],0)
        hf_quant(BLOCKS[1],0)
        h_mul(BLOCKS[4],0)
        up(BLOCKS[2],3)
        load_gate(BLOCKS[7])
        w_mix(3,0,1,"S")
        h_mul(BLOCKS[4],3)
        hf_quant(BLOCKS[3],0)
        h_turn(BLOCKS[0],1)
        h_mul(BLOCKS[2],3)
        h_turn(BLOCKS[2],0)
        up(BLOCKS[4],1)
        h_copy(BLOCKS[0],1,"S")
        up(BLOCKS[6],1)
        w_mix(3,1,1,"S")
        load_gate(BLOCKS[5])
        load_gate(BLOCKS[6])
        w_quant(3,0,0,512)
        up(BLOCKS[4],2)
        h_copy(BLOCKS[2],0,"S")
        h_mul(BLOCKS[4],1)
        hf_quant(BLOCKS[1],1)
        w_quant(3,1,0,512)
        h_turn(BLOCKS[2],1)
        h_mul(BLOCKS[6],1)
        load_down()
        h_turn(BLOCKS[4],0)
        up(BLOCKS[5],1)
        hm_mix(BLOCKS[1],0,"S")
        h_mul(BLOCKS[4],2)
        up(BLOCKS[7],1)
        up(BLOCKS[5],0)
        h_mul(BLOCKS[5],1)
        up(BLOCKS[5],3)
        h_mul(BLOCKS[7],1)
        hm_mix(BLOCKS[3],0,"S")
        h_copy(BLOCKS[2],1,"S")
        h_mul(BLOCKS[5],0)
        up(BLOCKS[5],2)
        hf_quant(BLOCKS[0],1)
        h_mul(BLOCKS[5],3)
        hf_quant(BLOCKS[2],0)
        up(BLOCKS[7],0)
        h_mul(BLOCKS[5],2)
        h_turn(BLOCKS[4],1)
        h_copy(BLOCKS[4],0,"S")
        h_mul(BLOCKS[7],0)
        hm_mix(BLOCKS[3],1,"S")
        load_lora()
        h_copy(BLOCKS[4],1,"S")
        h_turn(BLOCKS[5],0)
        hf_quant(BLOCKS[4],0)
        h_copy(BLOCKS[5],0,"V")
        up(BLOCKS[7],3)
        h_mul(BLOCKS[7],3)
        hf_quant(BLOCKS[5],0)
        la_widen(0)
        up(BLOCKS[7],2)
        up(BLOCKS[6],3)
        h_mul(BLOCKS[7],2)
        h_turn(BLOCKS[7],0)
        hf_quant(BLOCKS[2],1)
        h_mul(BLOCKS[6],3)
        h_turn(BLOCKS[5],1)
        hm_mix(BLOCKS[1],1,"S")
        up(BLOCKS[6],0)
        h_copy(BLOCKS[7],0,"V")
        up(BLOCKS[6],2)
        y_mul(0,0,1)
        h_copy(BLOCKS[5],1,"S")
        y_mul(0,1,1)
        la_widen(3)
        load_dz()
        h_turn(BLOCKS[7],1)
        h_mul(BLOCKS[6],2)
        hf_quant(BLOCKS[4],1)
        h_mul(BLOCKS[6],0)
        h_turn(BLOCKS[6],0)
        y_copy(0,0,1,"S")
        hm_quant(BLOCKS[1])
        hf_quant(BLOCKS[5],1)
        y_copy(0,1,1,"V")
        la_widen(2)
        dz_mix(0,"V")
        hf_quant(BLOCKS[7],0)
        la_widen(1)
        y_mul(0,2,0)
        h_copy(BLOCKS[6],0,"S")
        la_mix(0,"S")
        hm_mix(BLOCKS[0],0,"S")
        y_mul(0,0,0)
        h_copy(BLOCKS[7],1,"V")
        h_turn(BLOCKS[6],1)
        la_mix(1,"V")
        h_turn(BLOCKS[3],1)
        y_copy(0,2,0,"V")
        hm_quant(BLOCKS[3])
        y_mul(0,3,0)
        hf_quant(BLOCKS[6],0)
        y_copy(0,0,0,"V")
        y_mul(1,0,1)
        h_copy(BLOCKS[3],1,"S")
        y_copy(0,3,0,"S")
        hm_mix(BLOCKS[2],0,"V")
        hf_quant(BLOCKS[7],1)
        h_copy(BLOCKS[6],1,"S")
        hf_quant(BLOCKS[3],1)
        y_copy(1,0,1,"V")
        hm_mix(BLOCKS[2],1,"S")
        y_mul(0,3,1)
        y_mul(1,1,1)
        y_copy(1,1,1,"S")
        y_mul(1,1,0)
        y_copy(0,3,1,"V")
        hf_quant(BLOCKS[6],1)
        hm_quant(BLOCKS[2])
        y_mul(0,1,0)
        hm_mix(BLOCKS[0],1,"S")
        dz_mix(1,"V")
        y_copy(1,1,0,"V")
        y_copy(0,1,0,"S")
        y_mul(1,3,0)
        hm_mix(BLOCKS[7],0,"V")
        hm_quant(BLOCKS[0])
        dz_quant()
        y_mul(1,2,0)
        la_quant()
        hm_mix(BLOCKS[6],0,"V")
        hm_mix(BLOCKS[4],0,"V")
        y_copy(1,3,0,"S")
        hm_mix(BLOCKS[5],0,"V")
        z_mul(0)
        y_copy(1,2,0,"S")
        da_mul(1)
        y_mul(1,2,1)
        hm_mix(BLOCKS[7],1,"S")
        z_copy(0,"V")
        hm_mix(BLOCKS[5],1,"V")
        z_mul(1)
        da_copy(1,"S")
        hm_mix(BLOCKS[4],1,"S")
        hm_quant(BLOCKS[7])
        y_copy(1,2,1,"S")
        z_copy(1,"S")
        y_mul(1,3,1)
        hm_mix(BLOCKS[6],1,"V")
        hm_quant(BLOCKS[4])
        y_copy(1,3,1,"V")
        y_mul(1,0,0)
        hm_quant(BLOCKS[5])
        hm_quant(BLOCKS[6])
        da_mul(0)
        y_copy(1,0,0,"S")
        da_mul(3)
        da_mul(2)
        da_copy(0,"S")
        da_copy(3,"V")
        da_copy(2,"V")
        y_mul(0,2,1)
        y_copy(0,2,1,"S")
